import numpy as np
CORES = [2,10,118,126]
N = 4
def setup_inputs(rng):
    return {"x1": rng.standard_normal((N, 128, 3), dtype=np.float32), "x2": rng.standard_normal((N, 128, 1), dtype=np.float32), "x3": rng.standard_normal((N, 128, 4), dtype=np.float32), "x4": rng.standard_normal((N, 128, 2), dtype=np.float32)}
def reference(x1, x2, x3, x4):
    out = {}
    s = x1.sum(axis=0, dtype=np.float64).astype(x1.dtype)
    out["y1"] = np.broadcast_to(s, (N,) + s.shape)
    s = x2.sum(axis=0, dtype=np.float64).astype(x2.dtype)
    out["y2"] = np.broadcast_to(s, (N,) + s.shape)
    s = x3.sum(axis=0, dtype=np.float64).astype(x3.dtype)
    out["y3"] = np.broadcast_to(s, (N,) + s.shape)
    s = x4.sum(axis=0, dtype=np.float64).astype(x4.dtype)
    out["y4"] = np.broadcast_to(s, (N,) + s.shape)
    return out

@@ -1,0 +1,50 @@
+from concourse.bass import DstId, RemoteDMATransfer
+from concourse.mybir import AluOpType
+
+COLS = ((1, 0, 3), (2, 3, 4), (3, 4, 8), (4, 8, 10))
+WIDTH = 10
+
+SCRATCH = {
+    "own": ("sbuf", [128, WIDTH], "float32"),
+    "mate": ("sbuf", [128, WIDTH], "float32"),
+    "part": ("sbuf", [128, WIDTH], "float32"),
+}
+SEMAPHORES = ["loaded", "seeded", "arr1", "arr2", "sent", "add1", "add2"]
+
+
+def rank_program(g, core, T, topo):
+    rank = T.rank_of(core)
+    if rank is None:
+        return
+    S = T.sem
+    others = [c for c in T.cores if c != core]
+    mate = [c for c in others if topo.mates(topo.chip(core), topo.chip(c))][0]
+    peer = [c for c in others if topo.same_plane(topo.chip(core), topo.chip(c))][0]
+
+    queues = (g.sync, g.scalar, g.scalar, g.sync)
+    for q, (i, lo, hi) in zip(queues, COLS):
+        q.dma_start(T.own[:, lo:hi], T["x%d" % i][:]).then_inc(S.loaded, 16)
+    for q, (i, lo, hi) in zip(queues, COLS):
+        q.dma_start(T["y%d" % i][:], T["x%d" % i][:]).then_inc(S.seeded, 16)
+
+    g.wait_ge(S.loaded, 64)
+    rid, pid, _se = topo.addr(mate)
+    g.remote_dma(T.mate[:], T.own[:], remote_sem=S.arr1, local_sem=S.sent, pid=pid, routing_id=rid,
+                 dma_engine_mask=topo.mask(core, mate))
+    g.wait_ge(S.arr1, 8)
+
+    rid, pid, _se = topo.addr(peer)
+    g.remote_dma_fused([RemoteDMATransfer(dst_ids=[DstId(rid=rid, pnc=pid)], dma_engine_mask=topo.mask(core, peer),
+                                          remote_sem=S.arr2, srcs=[T.own[:], T.mate[:]], dsts=[T.part[:]],
+                                          alu_op=1)], local_sem=S.sent)
+
+    g.wait_ge(S.seeded, 64)
+    for i, lo, hi in COLS:
+        g.dma_start(T["y%d" % i][:], T.mate[:, lo:hi], accum_op=AluOpType.add).then_inc(S.add1, 16)
+    g.wait_ge(S.add1, 64)
+
+    g.wait_ge(S.arr2, 8)
+    for i, lo, hi in COLS:
+        g.dma_start(T["y%d" % i][:], T.part[:, lo:hi], accum_op=AluOpType.add).then_inc(S.add2, 16)
+    g.wait_ge(S.add2, 64)
+    g.wait_ge(S.sent, 16)

@@ -1,14 +1,15 @@
 from concourse.bass import DstId, RemoteDMATransfer
 from concourse.mybir import AluOpType
 
-COLS = ((1, 0, 3), (2, 3, 4), (3, 4, 8), (4, 8, 10))
-WIDTH = 10
+PLACE = ((3, "a", 0, 64), (1, "a", 64, 112), (2, "a", 112, 128), (4, "b", 0, 128))
+BLOCKS = (("a", 8, 0x0F), ("b", 2, 0xF0))
+PER_STEP = 8
 
-SCRATCH = {
-    "own": ("sbuf", [128, WIDTH], "float32"),
-    "mate": ("sbuf", [128, WIDTH], "float32"),
-    "part": ("sbuf", [128, WIDTH], "float32"),
-}
+SCRATCH = {}
+for blk_name, blk_width, blk_mask in BLOCKS:
+    SCRATCH["own_" + blk_name] = ("dram", [128, blk_width], "float32")
+    SCRATCH["mate_" + blk_name] = ("dram", [128, blk_width], "float32")
+    SCRATCH["part_" + blk_name] = ("dram", [128, blk_width], "float32")
 SEMAPHORES = ["loaded", "seeded", "arr1", "arr2", "sent", "add1", "add2"]
 
 
@@ -21,30 +22,32 @@ def rank_program(g, core, T, topo):
     mate = [c for c in others if topo.mates(topo.chip(core), topo.chip(c))][0]
     peer = [c for c in others if topo.same_plane(topo.chip(core), topo.chip(c))][0]
 
-    queues = (g.sync, g.scalar, g.scalar, g.sync)
-    for q, (i, lo, hi) in zip(queues, COLS):
-        q.dma_start(T.own[:, lo:hi], T["x%d" % i][:]).then_inc(S.loaded, 16)
-    for q, (i, lo, hi) in zip(queues, COLS):
+    queues = (g.sync, g.scalar, g.sync, g.scalar)
+    for q, (i, blk, lo, hi) in zip(queues, PLACE):
+        q.dma_start(T["own_" + blk][lo:hi, :], T["x%d" % i][:]).then_inc(S.loaded, 16)
+    for q, (i, blk, lo, hi) in zip(queues, PLACE):
         q.dma_start(T["y%d" % i][:], T["x%d" % i][:]).then_inc(S.seeded, 16)
 
     g.wait_ge(S.loaded, 64)
-    rid, pid, _se = topo.addr(mate)
-    g.remote_dma(T.mate[:], T.own[:], remote_sem=S.arr1, local_sem=S.sent, pid=pid, routing_id=rid,
-                 dma_engine_mask=topo.mask(core, mate))
-    g.wait_ge(S.arr1, 8)
+    rid, pid = topo.addr(mate)[0:2]
+    for blk, width, m in BLOCKS:
+        g.remote_dma(T["mate_" + blk][:], T["own_" + blk][:], remote_sem=S.arr1, local_sem=S.sent, pid=pid,
+                     routing_id=rid, dma_engine_mask=m)
+    g.wait_ge(S.arr1, PER_STEP)
 
-    rid, pid, _se = topo.addr(peer)
-    g.remote_dma_fused([RemoteDMATransfer(dst_ids=[DstId(rid=rid, pnc=pid)], dma_engine_mask=topo.mask(core, peer),
-                                          remote_sem=S.arr2, srcs=[T.own[:], T.mate[:]], dsts=[T.part[:]],
-                                          alu_op=1)], local_sem=S.sent)
+    rid, pid = topo.addr(peer)[0:2]
+    for blk, width, m in BLOCKS:
+        g.remote_dma_fused([RemoteDMATransfer(dst_ids=[DstId(rid=rid, pnc=pid)], dma_engine_mask=m, remote_sem=S.arr2,
+                                              srcs=[T["own_" + blk][:], T["mate_" + blk][:]],
+                                              dsts=[T["part_" + blk][:]], alu_op=1)], local_sem=S.sent)
 
     g.wait_ge(S.seeded, 64)
-    for i, lo, hi in COLS:
-        g.dma_start(T["y%d" % i][:], T.mate[:, lo:hi], accum_op=AluOpType.add).then_inc(S.add1, 16)
+    for i, blk, lo, hi in PLACE:
+        g.dma_start(T["y%d" % i][:], T["mate_" + blk][lo:hi, :], accum_op=AluOpType.add).then_inc(S.add1, 16)
     g.wait_ge(S.add1, 64)
 
-    g.wait_ge(S.arr2, 8)
-    for i, lo, hi in COLS:
-        g.dma_start(T["y%d" % i][:], T.part[:, lo:hi], accum_op=AluOpType.add).then_inc(S.add2, 16)
+    g.wait_ge(S.arr2, PER_STEP)
+    for i, blk, lo, hi in PLACE:
+        g.dma_start(T["y%d" % i][:], T["part_" + blk][lo:hi, :], accum_op=AluOpType.add).then_inc(S.add2, 16)
     g.wait_ge(S.add2, 64)
-    g.wait_ge(S.sent, 16)
+    g.wait_ge(S.sent, 2 * PER_STEP)

from concourse.bass import DstId, RemoteDMATransfer
from concourse.mybir import AluOpType

PLACE = ((3, "a", 0, 64), (1, "a", 64, 112), (2, "a", 112, 128), (4, "b", 0, 128))
BLOCKS = (("a", 8, 0x0F), ("b", 2, 0xF0))
PER_STEP = 8

SCRATCH = {}
for blk_name, blk_width, blk_mask in BLOCKS:
    SCRATCH["own_" + blk_name] = ("dram", [128, blk_width], "float32")
    SCRATCH["mate_" + blk_name] = ("dram", [128, blk_width], "float32")
    SCRATCH["part_" + blk_name] = ("dram", [128, blk_width], "float32")
SEMAPHORES = ["loaded", "seeded", "arr1", "arr2", "sent", "add1", "add2"]


def rank_program(g, core, T, topo):
    rank = T.rank_of(core)
    if rank is None:
        return
    S = T.sem
    others = [c for c in T.cores if c != core]
    mate = [c for c in others if topo.mates(topo.chip(core), topo.chip(c))][0]
    peer = [c for c in others if topo.same_plane(topo.chip(core), topo.chip(c))][0]

    queues = (g.sync, g.scalar, g.sync, g.scalar)
    for q, (i, blk, lo, hi) in zip(queues, PLACE):
        q.dma_start(T["own_" + blk][lo:hi, :], T["x%d" % i][:]).then_inc(S.loaded, 16)
    for q, (i, blk, lo, hi) in zip(queues, PLACE):
        q.dma_start(T["y%d" % i][:], T["x%d" % i][:]).then_inc(S.seeded, 16)

    g.wait_ge(S.loaded, 64)
    rid, pid = topo.addr(mate)[0:2]
    for blk, width, m in BLOCKS:
        g.remote_dma(T["mate_" + blk][:], T["own_" + blk][:], remote_sem=S.arr1, local_sem=S.sent, pid=pid,
                     routing_id=rid, dma_engine_mask=m)
    g.wait_ge(S.arr1, PER_STEP)

    rid, pid = topo.addr(peer)[0:2]
    for blk, width, m in BLOCKS:
        g.remote_dma_fused([RemoteDMATransfer(dst_ids=[DstId(rid=rid, pnc=pid)], dma_engine_mask=m, remote_sem=S.arr2,
                                              srcs=[T["own_" + blk][:], T["mate_" + blk][:]],
                                              dsts=[T["part_" + blk][:]], alu_op=1)], local_sem=S.sent)

    g.wait_ge(S.seeded, 64)
    for i, blk, lo, hi in PLACE:
        g.dma_start(T["y%d" % i][:], T["mate_" + blk][lo:hi, :], accum_op=AluOpType.add).then_inc(S.add1, 16)
    g.wait_ge(S.add1, 64)

    g.wait_ge(S.arr2, PER_STEP)
    for i, blk, lo, hi in PLACE:
        g.dma_start(T["y%d" % i][:], T["part_" + blk][lo:hi, :], accum_op=AluOpType.add).then_inc(S.add2, 16)
    g.wait_ge(S.add2, 64)
    g.wait_ge(S.sent, 2 * PER_STEP)
